import numpy as np
import ml_dtypes


def mxq(x, axis, fmt="e4m3"):
    dtype, down = {"e4m3": (ml_dtypes.float8_e4m3fn, 7), "e5m2": (ml_dtypes.float8_e5m2, 14)}[fmt]
    v = np.moveaxis(np.asarray(x, np.float32).astype(ml_dtypes.bfloat16).astype(np.float64), axis, -1)
    blocks = v.reshape(v.shape[:-1] + (-1, 32))
    amax = np.abs(blocks).max(-1, keepdims=True)
    byte = np.maximum(np.where(amax > 0, np.frexp(amax)[1] - 1 + 127, 0) - down, 1)
    scale = np.exp2(byte - 127.0)
    codes = (blocks / scale).astype(np.float32).astype(dtype).astype(np.float64)
    return np.moveaxis((codes * scale).reshape(v.shape), -1, axis)


WIDE = False


def mx_kscale(k):
    if not WIDE:
        return np.ones(k)
    levels = np.array([10, -10, 5, -5, 0])
    if k % 512:
        return np.exp2(np.random.permutation(np.resize(levels, k // 32))).repeat(32)
    a = np.empty((k // 512, 16))
    for p in range(k // 512):
        a[p, :8] = np.random.permutation(np.resize(levels, 8))
        for g in range(8):
            far = levels[np.abs(levels - a[p, g]) >= 10]
            a[p, g + 8] = far[np.random.randint(len(far))]
    return np.exp2(a.ravel()).repeat(32)


def f64(x):
    return np.asarray(x).astype(np.float64)


def striped(idx):
    return np.tile(np.asarray(idx).reshape(-1, 16).T, (8, 1)).astype(np.uint16)


def unstriped(offs):
    return offs[:16].T.reshape(-1).astype(np.int64)


B, N, T, D, DV, NQ = 1, 2048, 4096, 512, 512, 128
PAGE = 128


def setup_inputs():
    n = np.random.standard_normal
    pages = np.random.permutation(T // PAGE)[:B * N // PAGE]
    idx = (pages[:, None] * PAGE + np.arange(PAGE)[None, :]).reshape(-1)
    s = mx_kscale(D)[:, None]
    u = np.ones(T)
    u[idx] = mx_kscale(B * N)
    r = np.random.uniform(0.5, 2.0, T)
    raw = n((D, T)) / s / (u * r)
    return {
        "qT": (n((B, D, NQ)) * s * (0.90 / np.sqrt(D))).astype(np.float32),
        "cT": raw.astype(np.float32),
        "ts": np.tile(u * r, (128, 1)).astype(np.float32),
        "ch": np.tile(s[:, 0] * np.random.uniform(0.5, 2.0, D), (128, 1)).astype(np.float32),
        "offs": striped(idx),
    }


def reference(qT, cT, ts, ch, offs):
    idx = unstriped(offs)
    c = f64(cT)
    pick = lambda x: x[:, idx].reshape(x.shape[0], B, N).transpose(1, 0, 2)
    q = f64(qT)
    score = mxq(q, 1, "e4m3").transpose(0, 2, 1) @ mxq(pick(c), 1, "e4m3")
    score = score * pick(f64(ts))[:, :1, :]
    m = score.max(-1, keepdims=True)
    p = np.exp(score - m)
    total = p.sum(-1, keepdims=True)
    w = p * pick(f64(ts))[:, :1, :]
    y = mxq(w, 2, "e4m3") @ mxq(pick(c).transpose(0, 2, 1), 1, "e4m3")
    y = y / total
    y = y * f64(ch)[:1]
    return y

@@ -1,0 +1,255 @@
+from contextlib import ExitStack
+
+import concourse.mybir as mybir
+from concourse.masks import make_identity
+
+F32 = mybir.dt.float32
+BF16 = mybir.dt.bfloat16
+U32 = mybir.dt.uint32
+U16 = mybir.dt.uint16
+U8 = mybir.dt.uint8
+FP8X4 = mybir.dt.float8_e4m3fn_x4
+COPY = mybir.ActivationFunctionType.Copy
+EXP = mybir.ActivationFunctionType.Exp
+MULT = mybir.AluOpType.mult
+MIN = mybir.AluOpType.min
+ADD = mybir.AluOpType.add
+AXIS_X = mybir.AxisListType.X
+
+P = 128
+PACK = 4
+D = 512
+T = 4096
+N = 2048
+NQ = 128
+PASS = 512
+CHUNKS = N // PASS
+
+FLOPS = 4 * NQ * N * D
+BYTES = 4 * (D * NQ + D * T + T + D + NQ * D) + 2 * N
+
+
+def tile_attend_mla_long_kernel(tc, qT, cT, ts, ch, offs, out):
+    nc = tc.nc
+    with ExitStack() as ctx:
+        hold = ctx.enter_context(tc.tile_pool(name="hold", bufs=1))
+        psum = ctx.enter_context(tc.psum_pool(name="psum", bufs=1))
+
+        offsets = hold.tile([P, N // 16], U16, name="offsets")
+        nc.sync.dma_start(offsets[:], offs)
+        planes = []
+        rows = cT.rearrange("(p t) n -> t p n", t=PACK)
+        for t in range(PACK):
+            plane = hold.tile([P, T], F32, name=f"plane{t}")
+            nc.sync.dma_start(out=plane[:], in_=rows[t])
+            planes.append(plane)
+        q_raw = hold.tile([P, PACK, NQ], F32, name="q_raw")
+        nc.sync.dma_start(out=q_raw[:], in_=qT[0].rearrange("(p t) q -> p t q", t=PACK))
+        ch_sb = hold.tile([P, D], F32, name="ch_sb")
+        nc.sync.dma_start(out=ch_sb[:], in_=ch)
+
+        warm = hold.tile([P, 1], F32, name="warm")
+        nc.vector.memset(warm[:], 0.0)
+        warm_out = hold.tile([P, 1], F32, name="warm_out")
+        nc.scalar.activation(warm_out[:], warm[:], EXP)
+        ts_row = hold.tile([P, T], F32, name="ts_row")
+        nc.vector.memset(ts_row[:], 0.0)
+        nc.scalar.dma_start(out=ts_row[0:1, :], in_=ts[0:1, :])
+        ident = hold.tile([P, P], F32, name="ident")
+        make_identity(nc, ident[:])
+
+        g01 = hold.tile([P, 2, N], F32, name="g01")
+        g23 = hold.tile([P, 2, N], F32, name="g23")
+        pairs = (g01, g23)
+        k_grouped = hold.tile([P, N, PACK], BF16, name="k_grouped", align_bytes=64)
+        k_codes = hold.tile([P, N], U32, name="k_codes", align_bytes=64)
+        k_scales = hold.tile([P, N], U8, name="k_scales", align_bytes=64)
+        v_grouped = hold.tile([P, CHUNKS, D, PACK], BF16, name="v_grouped", align_bytes=64)
+        v_codes = hold.tile([P, CHUNKS, D], U32, name="v_codes", align_bytes=64)
+        v_scales = hold.tile([P, CHUNKS, D], U8, name="v_scales", align_bytes=64)
+
+        def gather(t, first, last):
+            nc.vector.tensor_copy(
+                pairs[t // 2][:, t % 2, first:last],
+                planes[t][:].indirect(offsets[:, first // 16 : last // 16]),
+            )
+
+        def turn(t, j):
+            bank = psum.tile([P, PACK, P], F32, name="turned", tag="turned", bufs=3)
+            for u in range(PACK):
+                nc.tensor.transpose(
+                    bank[:, u, :],
+                    pairs[t // 2][:, t % 2, PASS * j + u : PASS * (j + 1) : PACK],
+                    ident[:],
+                )
+            nc.scalar.copy(
+                v_grouped[:, j, t * P : (t + 1) * P, :], bank[:].rearrange("s u p -> s p u")
+            )
+
+        def quantize_v(t, j):
+            e = slice(t * P, (t + 1) * P)
+            nc.vector.quantize_mx(
+                out=v_codes[:, j, e].bitcast(FP8X4),
+                scales=v_scales[:, j, e],
+                in_=v_grouped[:, j, e, :].rearrange("s e u -> s (e u)"),
+            )
+
+        def insert(engine_copy, half, j):
+            n = slice(PASS * j, PASS * (j + 1))
+            engine_copy(
+                k_grouped[:, n, 2 * half : 2 * half + 2],
+                pairs[half][:, :, n].rearrange("p t n -> p n t"),
+            )
+
+        gather(0, 0, 1024)
+        gather(0, 1024, 2048)
+        for j in range(CHUNKS):
+            turn(0, j)
+
+        ts_list = hold.tile([P, N], F32, name="ts_list")
+        nc.vector.tensor_copy(ts_list[:], ts_row[:].indirect(offsets[:]))
+        ts_col = hold.tile([P, CHUNKS, PACK], F32, name="ts_col")
+        neg_ts = hold.tile([P, CHUNKS, PACK, P], F32, name="neg_ts")
+        for j in range(CHUNKS):
+            bank = psum.tile([P, PACK, P], F32, name="ts_turned", tag="turned", bufs=3)
+            for u in range(PACK):
+                nc.tensor.transpose(
+                    bank[:, u, :], ts_list[:, PASS * j + u : PASS * (j + 1) : PACK], ident[:]
+                )
+            nc.scalar.copy(ts_col[:, j, :], bank[:, :, 0])
+        for j in range(CHUNKS):
+            bank = psum.tile([P, PACK, P], F32, name="ts_spread", tag="turned", bufs=3)
+            for u in range(PACK):
+                nc.tensor.transpose(
+                    bank[:, u, :], ts_col[:, j, u : u + 1].to_broadcast([P, P]), ident[:]
+                )
+            nc.scalar.activation(neg_ts[:, j], bank[:], COPY, scale=-1.0)
+
+        gather(1, 0, 1024)
+        gather(1, 1024, 2048)
+        for j in range(CHUNKS):
+            insert(nc.vector.tensor_copy if j < 2 else nc.scalar.copy, 0, j)
+        for j in range(CHUNKS):
+            turn(1, j)
+        gather(2, 0, 1024)
+        gather(2, 1024, 2048)
+        for j in range(CHUNKS):
+            turn(2, j)
+        for t in range(2):
+            for j in range(CHUNKS):
+                quantize_v(t, j)
+
+        for j in range(CHUNKS):
+            gather(3, PASS * j, PASS * (j + 1))
+            insert(nc.scalar.copy, 1, j)
+
+        q_grouped = hold.tile([P, NQ, PACK], BF16, name="q_grouped", align_bytes=64)
+        q_codes = hold.tile([P, NQ], U32, name="q_codes", align_bytes=64)
+        q_scales = hold.tile([P, NQ], U8, name="q_scales", align_bytes=64)
+        nc.vector.tensor_copy(q_grouped[:], q_raw[:].rearrange("p t q -> p q t"))
+        nc.vector.quantize_mx(
+            out=q_codes[:].bitcast(FP8X4),
+            scales=q_scales[:],
+            in_=q_grouped[:].rearrange("p q t -> p (q t)"),
+        )
+
+        neg_a = hold.tile([P, CHUNKS, PACK, P], F32, name="neg_a")
+        mins = hold.tile([P, CHUNKS], F32, name="mins")
+        neg_m = hold.tile([P, 1], F32, name="neg_m")
+
+        def score(j):
+            n = slice(PASS * j, PASS * (j + 1))
+            nc.vector.quantize_mx(
+                out=k_codes[:, n].bitcast(FP8X4),
+                scales=k_scales[:, n],
+                in_=k_grouped[:, n, :].rearrange("p n t -> p (n t)"),
+            )
+            bank = psum.tile([P, PASS], F32, name="score", tag="score", bufs=2)
+            nc.tensor.matmul_mx(
+                bank[:],
+                lhsT=q_codes[:].bitcast(FP8X4),
+                lhsT_scale=q_scales[:],
+                rhs=k_codes[:, n].bitcast(FP8X4),
+                rhs_scale=k_scales[:, n],
+                start=True,
+                stop=True,
+            )
+            return bank
+
+        def weigh(j, bank):
+            nc.vector.tensor_tensor(
+                neg_a[:, j], bank[:].rearrange("q (s u) -> q u s", u=PACK), neg_ts[:, j], MULT
+            )
+
+        def least(j):
+            nc.vector.tensor_reduce(
+                mins[:, j : j + 1],
+                neg_a[:, j].rearrange("q u s -> q (u s)"),
+                axis=AXIS_X,
+                op=MIN,
+            )
+
+        banks = [score(0)]
+        for j in range(CHUNKS):
+            if j + 1 < CHUNKS:
+                banks.append(score(j + 1))
+            weigh(j, banks[j])
+            turn(3, j)
+            quantize_v(2, j)
+            least(j)
+        nc.vector.tensor_reduce(neg_m[:], mins[:], axis=AXIS_X, op=MIN)
+
+        p_sb = hold.tile([P, CHUNKS, PACK, P], F32, name="p_sb")
+        sums = hold.tile([P, CHUNKS], F32, name="sums")
+        w_grouped = hold.tile([P, CHUNKS, NQ, PACK], BF16, name="w_grouped", align_bytes=64)
+        w_codes = hold.tile([P, CHUNKS, NQ], U32, name="w_codes", align_bytes=64)
+        w_scales = hold.tile([P, CHUNKS, NQ], U8, name="w_scales", align_bytes=64)
+        for j in range(CHUNKS):
+            nc.scalar.activation(
+                p_sb[:, j], neg_a[:, j], EXP, bias=neg_m[:], scale=-1.0, accum_out=sums[:, j : j + 1]
+            )
+        for j in range(CHUNKS):
+            quantize_v(3, j)
+        y = psum.tile([P, D], F32, name="y", tag="y", bufs=1)
+        for j in range(CHUNKS):
+            bank = psum.tile([P, PACK, P], F32, name="p_turned", tag="p_turned", bufs=2)
+            for u in range(PACK):
+                nc.tensor.transpose(bank[:, u, :], p_sb[:, j, u, :], ident[:])
+            nc.vector.tensor_tensor(
+                w_grouped[:, j],
+                bank[:].rearrange("s u q -> s q u"),
+                ts_col[:, j, :].unsqueeze(1).to_broadcast([P, NQ, PACK]),
+                MULT,
+            )
+            nc.vector.quantize_mx(
+                out=w_codes[:, j, :].bitcast(FP8X4),
+                scales=w_scales[:, j, :],
+                in_=w_grouped[:, j].rearrange("s q u -> s (q u)"),
+            )
+            nc.tensor.matmul_mx(
+                y[:],
+                lhsT=w_codes[:, j, :].bitcast(FP8X4),
+                lhsT_scale=w_scales[:, j, :],
+                rhs=v_codes[:, j, :].bitcast(FP8X4),
+                rhs_scale=v_scales[:, j, :],
+                start=(j == 0),
+                stop=(j == CHUNKS - 1),
+            )
+        total = hold.tile([P, 1], F32, name="total")
+        nc.vector.tensor_reduce(total[:], sums[:], axis=AXIS_X, op=ADD)
+        share = hold.tile([P, 1], F32, name="share")
+        nc.vector.reciprocal(share[:], total[:])
+
+        for h, queue in enumerate((nc.sync, nc.scalar)):
+            half = P // 2
+            e = slice(h * D // 2, (h + 1) * D // 2)
+            result = hold.tile([P, half, PACK], F32, name=f"result{h}")
+            nc.vector.scalar_tensor_tensor(
+                out=result[:],
+                in0=y[:].rearrange("q (t p) -> q p t", t=PACK)[:, h * half : (h + 1) * half, :],
+                scalar=share[:],
+                in1=ch_sb[:, e].rearrange("q (p t) -> q p t", t=PACK),
+                op0=MULT,
+                op1=MULT,
+            )
+            queue.dma_start(out=out[0][:, e], in_=result[:].rearrange("q p t -> q (p t)"))

@@ -37,12 +37,17 @@ def tile_attend_mla_long_kernel(tc, qT, cT, ts, ch, offs, out):
 
         offsets = hold.tile([P, N // 16], U16, name="offsets")
         nc.sync.dma_start(offsets[:], offs)
-        planes = []
         rows = cT.rearrange("(p t) n -> t p n", t=PACK)
-        for t in range(PACK):
-            plane = hold.tile([P, T], F32, name=f"plane{t}")
-            nc.sync.dma_start(out=plane[:], in_=rows[t])
-            planes.append(plane)
+        planes = [hold.tile([P, T], F32, name=f"plane{t}") for t in range(PACK)]
+        ts_row = hold.tile([P, T], F32, name="ts_row")
+        nc.sync.dma_start(out=planes[0][:], in_=rows[0])
+        nc.vector.memset(ts_row[:, 0 : T // 2], 0.0)
+        nc.gpsimd.memset(ts_row[:, T // 2 : T], 0.0)
+        for t in range(1, PACK):
+            nc.vector.memset(planes[t][:, 0:8], 0.0)
+        nc.sync.dma_start(out=ts_row[0:1, :], in_=ts[0:1, :])
+        for t in range(1, PACK):
+            nc.sync.dma_start(out=planes[t][:], in_=rows[t])
         q_raw = hold.tile([P, PACK, NQ], F32, name="q_raw")
         nc.sync.dma_start(out=q_raw[:], in_=qT[0].rearrange("(p t) q -> p t q", t=PACK))
         ch_sb = hold.tile([P, D], F32, name="ch_sb")
@@ -52,9 +57,6 @@ def tile_attend_mla_long_kernel(tc, qT, cT, ts, ch, offs, out):
         nc.vector.memset(warm[:], 0.0)
         warm_out = hold.tile([P, 1], F32, name="warm_out")
         nc.scalar.activation(warm_out[:], warm[:], EXP)
-        ts_row = hold.tile([P, T], F32, name="ts_row")
-        nc.vector.memset(ts_row[:], 0.0)
-        nc.scalar.dma_start(out=ts_row[0:1, :], in_=ts[0:1, :])
         ident = hold.tile([P, P], F32, name="ident")
         make_identity(nc, ident[:])
 
@@ -86,8 +88,8 @@ def tile_attend_mla_long_kernel(tc, qT, cT, ts, ch, offs, out):
                 v_grouped[:, j, t * P : (t + 1) * P, :], bank[:].rearrange("s u p -> s p u")
             )
 
-        def quantize_v(t, j):
-            e = slice(t * P, (t + 1) * P)
+        def quantize_v(half, j):
+            e = slice(half * 2 * P, (half + 1) * 2 * P)
             nc.vector.quantize_mx(
                 out=v_codes[:, j, e].bitcast(FP8X4),
                 scales=v_scales[:, j, e],
@@ -128,16 +130,15 @@ def tile_attend_mla_long_kernel(tc, qT, cT, ts, ch, offs, out):
         gather(1, 0, 1024)
         gather(1, 1024, 2048)
         for j in range(CHUNKS):
-            insert(nc.vector.tensor_copy if j < 2 else nc.scalar.copy, 0, j)
+            insert(nc.vector.tensor_copy, 0, j)
         for j in range(CHUNKS):
             turn(1, j)
         gather(2, 0, 1024)
         gather(2, 1024, 2048)
         for j in range(CHUNKS):
             turn(2, j)
-        for t in range(2):
-            for j in range(CHUNKS):
-                quantize_v(t, j)
+        for j in range(CHUNKS):
+            quantize_v(0, j)
 
         for j in range(CHUNKS):
             gather(3, PASS * j, PASS * (j + 1))
@@ -195,7 +196,6 @@ def tile_attend_mla_long_kernel(tc, qT, cT, ts, ch, offs, out):
                 banks.append(score(j + 1))
             weigh(j, banks[j])
             turn(3, j)
-            quantize_v(2, j)
             least(j)
         nc.vector.tensor_reduce(neg_m[:], mins[:], axis=AXIS_X, op=MIN)
 
@@ -209,7 +209,7 @@ def tile_attend_mla_long_kernel(tc, qT, cT, ts, ch, offs, out):
                 p_sb[:, j], neg_a[:, j], EXP, bias=neg_m[:], scale=-1.0, accum_out=sums[:, j : j + 1]
             )
         for j in range(CHUNKS):
-            quantize_v(3, j)
+            quantize_v(1, j)
         y = psum.tile([P, D], F32, name="y", tag="y", bufs=1)
         for j in range(CHUNKS):
             bank = psum.tile([P, PACK, P], F32, name="p_turned", tag="p_turned", bufs=2)

@@ -40,12 +40,14 @@ def tile_attend_mla_long_kernel(tc, qT, cT, ts, ch, offs, out):
         rows = cT.rearrange("(p t) n -> t p n", t=PACK)
         planes = [hold.tile([P, T], F32, name=f"plane{t}") for t in range(PACK)]
         ts_row = hold.tile([P, T], F32, name="ts_row")
-        nc.sync.dma_start(out=planes[0][:], in_=rows[0])
-        nc.vector.memset(ts_row[:, 0 : T // 2], 0.0)
-        nc.gpsimd.memset(ts_row[:, T // 2 : T], 0.0)
+        nc.sync.dma_start(out=planes[0][:, 0 : T // 2], in_=rows[0][:, 0 : T // 2])
+        nc.vector.memset(ts_row[:, 0:2816], 0.0)
+        nc.gpsimd.memset(ts_row[:, 2816:T], 0.0)
+        nc.vector.memset(planes[0][:, T // 2 : T // 2 + 8], 0.0)
         for t in range(1, PACK):
             nc.vector.memset(planes[t][:, 0:8], 0.0)
         nc.sync.dma_start(out=ts_row[0:1, :], in_=ts[0:1, :])
+        nc.sync.dma_start(out=planes[0][:, T // 2 : T], in_=rows[0][:, T // 2 : T])
         for t in range(1, PACK):
             nc.sync.dma_start(out=planes[t][:], in_=rows[t])
         q_raw = hold.tile([P, PACK, NQ], F32, name="q_raw")
@@ -77,7 +79,7 @@ def tile_attend_mla_long_kernel(tc, qT, cT, ts, ch, offs, out):
             )
 
         def turn(t, j):
-            bank = psum.tile([P, PACK, P], F32, name="turned", tag="turned", bufs=3)
+            bank = psum.tile([P, PACK, P], F32, name="turned", tag="turned", bufs=4)
             for u in range(PACK):
                 nc.tensor.transpose(
                     bank[:, u, :],
@@ -103,29 +105,33 @@ def tile_attend_mla_long_kernel(tc, qT, cT, ts, ch, offs, out):
                 pairs[half][:, :, n].rearrange("p t n -> p n t"),
             )
 
-        gather(0, 0, 1024)
-        gather(0, 1024, 2048)
-        for j in range(CHUNKS):
-            turn(0, j)
-
         ts_list = hold.tile([P, N], F32, name="ts_list")
-        nc.vector.tensor_copy(ts_list[:], ts_row[:].indirect(offsets[:]))
+        for h in range(2):
+            nc.vector.tensor_copy(
+                ts_list[:, h * 1024 : (h + 1) * 1024],
+                ts_row[:].indirect(offsets[:, h * 64 : (h + 1) * 64]),
+            )
         ts_col = hold.tile([P, CHUNKS, PACK], F32, name="ts_col")
         neg_ts = hold.tile([P, CHUNKS, PACK, P], F32, name="neg_ts")
         for j in range(CHUNKS):
-            bank = psum.tile([P, PACK, P], F32, name="ts_turned", tag="turned", bufs=3)
+            bank = psum.tile([P, PACK, P], F32, name="ts_turned", tag="turned", bufs=4)
             for u in range(PACK):
                 nc.tensor.transpose(
                     bank[:, u, :], ts_list[:, PASS * j + u : PASS * (j + 1) : PACK], ident[:]
                 )
             nc.scalar.copy(ts_col[:, j, :], bank[:, :, 0])
         for j in range(CHUNKS):
-            bank = psum.tile([P, PACK, P], F32, name="ts_spread", tag="turned", bufs=3)
+            bank = psum.tile([P, PACK, P], F32, name="ts_spread", tag="turned", bufs=4)
             for u in range(PACK):
                 nc.tensor.transpose(
                     bank[:, u, :], ts_col[:, j, u : u + 1].to_broadcast([P, P]), ident[:]
                 )
             nc.scalar.activation(neg_ts[:, j], bank[:], COPY, scale=-1.0)
+
+        gather(0, 0, 1024)
+        gather(0, 1024, 2048)
+        for j in range(CHUNKS):
+            turn(0, j)
 
         gather(1, 0, 1024)
         gather(1, 1024, 2048)
@@ -165,7 +171,7 @@ def tile_attend_mla_long_kernel(tc, qT, cT, ts, ch, offs, out):
                 scales=k_scales[:, n],
                 in_=k_grouped[:, n, :].rearrange("p n t -> p (n t)"),
             )
-            bank = psum.tile([P, PASS], F32, name="score", tag="score", bufs=2)
+            bank = psum.tile([P, PASS], F32, name="score", tag="score", bufs=3)
             nc.tensor.matmul_mx(
                 bank[:],
                 lhsT=q_codes[:].bitcast(FP8X4),
@@ -190,13 +196,21 @@ def tile_attend_mla_long_kernel(tc, qT, cT, ts, ch, offs, out):
                 op=MIN,
             )
 
-        banks = [score(0)]
-        for j in range(CHUNKS):
-            if j + 1 < CHUNKS:
-                banks.append(score(j + 1))
-            weigh(j, banks[j])
-            turn(3, j)
-            least(j)
+        banks = [score(0), score(1)]
+        weigh(0, banks[0])
+        turn(3, 0)
+        banks.append(score(2))
+        least(0)
+        weigh(1, banks[1])
+        turn(3, 1)
+        banks.append(score(3))
+        least(1)
+        weigh(2, banks[2])
+        turn(3, 2)
+        least(2)
+        weigh(3, banks[3])
+        turn(3, 3)
+        least(3)
         nc.vector.tensor_reduce(neg_m[:], mins[:], axis=AXIS_X, op=MIN)
 
         p_sb = hold.tile([P, CHUNKS, PACK, P], F32, name="p_sb")
@@ -211,16 +225,22 @@ def tile_attend_mla_long_kernel(tc, qT, cT, ts, ch, offs, out):
         for j in range(CHUNKS):
             quantize_v(1, j)
         y = psum.tile([P, D], F32, name="y", tag="y", bufs=1)
-        for j in range(CHUNKS):
-            bank = psum.tile([P, PACK, P], F32, name="p_turned", tag="p_turned", bufs=2)
+
+        def turn_p(j):
+            bank = psum.tile([P, PACK, P], F32, name="p_turned", tag="turned", bufs=4)
             for u in range(PACK):
                 nc.tensor.transpose(bank[:, u, :], p_sb[:, j, u, :], ident[:])
+            return bank
+
+        def weights(j, bank):
             nc.vector.tensor_tensor(
                 w_grouped[:, j],
                 bank[:].rearrange("s u q -> s q u"),
                 ts_col[:, j, :].unsqueeze(1).to_broadcast([P, NQ, PACK]),
                 MULT,
             )
+
+        def product(j):
             nc.vector.quantize_mx(
                 out=w_codes[:, j, :].bitcast(FP8X4),
                 scales=w_scales[:, j, :],
@@ -235,9 +255,21 @@ def tile_attend_mla_long_kernel(tc, qT, cT, ts, ch, offs, out):
                 start=(j == 0),
                 stop=(j == CHUNKS - 1),
             )
+
         total = hold.tile([P, 1], F32, name="total")
-        nc.vector.tensor_reduce(total[:], sums[:], axis=AXIS_X, op=ADD)
         share = hold.tile([P, 1], F32, name="share")
+        turned = [turn_p(0), turn_p(1)]
+        weights(0, turned[0])
+        turned.append(turn_p(2))
+        weights(1, turned[1])
+        product(0)
+        turned.append(turn_p(3))
+        weights(2, turned[2])
+        product(1)
+        weights(3, turned[3])
+        product(2)
+        nc.vector.tensor_reduce(total[:], sums[:], axis=AXIS_X, op=ADD)
+        product(3)
         nc.vector.reciprocal(share[:], total[:])
 
         for h, queue in enumerate((nc.sync, nc.scalar)):

from contextlib import ExitStack

import concourse.mybir as mybir
from concourse.masks import make_identity

F32 = mybir.dt.float32
BF16 = mybir.dt.bfloat16
U32 = mybir.dt.uint32
U16 = mybir.dt.uint16
U8 = mybir.dt.uint8
FP8X4 = mybir.dt.float8_e4m3fn_x4
COPY = mybir.ActivationFunctionType.Copy
EXP = mybir.ActivationFunctionType.Exp
MULT = mybir.AluOpType.mult
MIN = mybir.AluOpType.min
ADD = mybir.AluOpType.add
AXIS_X = mybir.AxisListType.X

P = 128
PACK = 4
D = 512
T = 4096
N = 2048
NQ = 128
PASS = 512
CHUNKS = N // PASS

FLOPS = 4 * NQ * N * D
BYTES = 4 * (D * NQ + D * T + T + D + NQ * D) + 2 * N


def tile_attend_mla_long_kernel(tc, qT, cT, ts, ch, offs, out):
    nc = tc.nc
    with ExitStack() as ctx:
        hold = ctx.enter_context(tc.tile_pool(name="hold", bufs=1))
        psum = ctx.enter_context(tc.psum_pool(name="psum", bufs=1))

        offsets = hold.tile([P, N // 16], U16, name="offsets")
        nc.sync.dma_start(offsets[:], offs)
        rows = cT.rearrange("(p t) n -> t p n", t=PACK)
        planes = [hold.tile([P, T], F32, name=f"plane{t}") for t in range(PACK)]
        ts_row = hold.tile([P, T], F32, name="ts_row")
        nc.sync.dma_start(out=planes[0][:, 0 : T // 2], in_=rows[0][:, 0 : T // 2])
        nc.vector.memset(ts_row[:, 0:2816], 0.0)
        nc.gpsimd.memset(ts_row[:, 2816:T], 0.0)
        nc.vector.memset(planes[0][:, T // 2 : T // 2 + 8], 0.0)
        for t in range(1, PACK):
            nc.vector.memset(planes[t][:, 0:8], 0.0)
        nc.sync.dma_start(out=ts_row[0:1, :], in_=ts[0:1, :])
        nc.sync.dma_start(out=planes[0][:, T // 2 : T], in_=rows[0][:, T // 2 : T])
        for t in range(1, PACK):
            nc.sync.dma_start(out=planes[t][:], in_=rows[t])
        q_raw = hold.tile([P, PACK, NQ], F32, name="q_raw")
        nc.sync.dma_start(out=q_raw[:], in_=qT[0].rearrange("(p t) q -> p t q", t=PACK))
        ch_sb = hold.tile([P, D], F32, name="ch_sb")
        nc.sync.dma_start(out=ch_sb[:], in_=ch)

        warm = hold.tile([P, 1], F32, name="warm")
        nc.vector.memset(warm[:], 0.0)
        warm_out = hold.tile([P, 1], F32, name="warm_out")
        nc.scalar.activation(warm_out[:], warm[:], EXP)
        ident = hold.tile([P, P], F32, name="ident")
        make_identity(nc, ident[:])

        g01 = hold.tile([P, 2, N], F32, name="g01")
        g23 = hold.tile([P, 2, N], F32, name="g23")
        pairs = (g01, g23)
        k_grouped = hold.tile([P, N, PACK], BF16, name="k_grouped", align_bytes=64)
        k_codes = hold.tile([P, N], U32, name="k_codes", align_bytes=64)
        k_scales = hold.tile([P, N], U8, name="k_scales", align_bytes=64)
        v_grouped = hold.tile([P, CHUNKS, D, PACK], BF16, name="v_grouped", align_bytes=64)
        v_codes = hold.tile([P, CHUNKS, D], U32, name="v_codes", align_bytes=64)
        v_scales = hold.tile([P, CHUNKS, D], U8, name="v_scales", align_bytes=64)

        def gather(t, first, last):
            nc.vector.tensor_copy(
                pairs[t // 2][:, t % 2, first:last],
                planes[t][:].indirect(offsets[:, first // 16 : last // 16]),
            )

        def turn(t, j):
            bank = psum.tile([P, PACK, P], F32, name="turned", tag="turned", bufs=4)
            for u in range(PACK):
                nc.tensor.transpose(
                    bank[:, u, :],
                    pairs[t // 2][:, t % 2, PASS * j + u : PASS * (j + 1) : PACK],
                    ident[:],
                )
            nc.scalar.copy(
                v_grouped[:, j, t * P : (t + 1) * P, :], bank[:].rearrange("s u p -> s p u")
            )

        def quantize_v(half, j):
            e = slice(half * 2 * P, (half + 1) * 2 * P)
            nc.vector.quantize_mx(
                out=v_codes[:, j, e].bitcast(FP8X4),
                scales=v_scales[:, j, e],
                in_=v_grouped[:, j, e, :].rearrange("s e u -> s (e u)"),
            )

        def insert(engine_copy, half, j):
            n = slice(PASS * j, PASS * (j + 1))
            engine_copy(
                k_grouped[:, n, 2 * half : 2 * half + 2],
                pairs[half][:, :, n].rearrange("p t n -> p n t"),
            )

        ts_list = hold.tile([P, N], F32, name="ts_list")
        for h in range(2):
            nc.vector.tensor_copy(
                ts_list[:, h * 1024 : (h + 1) * 1024],
                ts_row[:].indirect(offsets[:, h * 64 : (h + 1) * 64]),
            )
        ts_col = hold.tile([P, CHUNKS, PACK], F32, name="ts_col")
        neg_ts = hold.tile([P, CHUNKS, PACK, P], F32, name="neg_ts")
        for j in range(CHUNKS):
            bank = psum.tile([P, PACK, P], F32, name="ts_turned", tag="turned", bufs=4)
            for u in range(PACK):
                nc.tensor.transpose(
                    bank[:, u, :], ts_list[:, PASS * j + u : PASS * (j + 1) : PACK], ident[:]
                )
            nc.scalar.copy(ts_col[:, j, :], bank[:, :, 0])
        for j in range(CHUNKS):
            bank = psum.tile([P, PACK, P], F32, name="ts_spread", tag="turned", bufs=4)
            for u in range(PACK):
                nc.tensor.transpose(
                    bank[:, u, :], ts_col[:, j, u : u + 1].to_broadcast([P, P]), ident[:]
                )
            nc.scalar.activation(neg_ts[:, j], bank[:], COPY, scale=-1.0)

        gather(0, 0, 1024)
        gather(0, 1024, 2048)
        for j in range(CHUNKS):
            turn(0, j)

        gather(1, 0, 1024)
        gather(1, 1024, 2048)
        for j in range(CHUNKS):
            insert(nc.vector.tensor_copy, 0, j)
        for j in range(CHUNKS):
            turn(1, j)
        gather(2, 0, 1024)
        gather(2, 1024, 2048)
        for j in range(CHUNKS):
            turn(2, j)
        for j in range(CHUNKS):
            quantize_v(0, j)

        for j in range(CHUNKS):
            gather(3, PASS * j, PASS * (j + 1))
            insert(nc.scalar.copy, 1, j)

        q_grouped = hold.tile([P, NQ, PACK], BF16, name="q_grouped", align_bytes=64)
        q_codes = hold.tile([P, NQ], U32, name="q_codes", align_bytes=64)
        q_scales = hold.tile([P, NQ], U8, name="q_scales", align_bytes=64)
        nc.vector.tensor_copy(q_grouped[:], q_raw[:].rearrange("p t q -> p q t"))
        nc.vector.quantize_mx(
            out=q_codes[:].bitcast(FP8X4),
            scales=q_scales[:],
            in_=q_grouped[:].rearrange("p q t -> p (q t)"),
        )

        neg_a = hold.tile([P, CHUNKS, PACK, P], F32, name="neg_a")
        mins = hold.tile([P, CHUNKS], F32, name="mins")
        neg_m = hold.tile([P, 1], F32, name="neg_m")

        def score(j):
            n = slice(PASS * j, PASS * (j + 1))
            nc.vector.quantize_mx(
                out=k_codes[:, n].bitcast(FP8X4),
                scales=k_scales[:, n],
                in_=k_grouped[:, n, :].rearrange("p n t -> p (n t)"),
            )
            bank = psum.tile([P, PASS], F32, name="score", tag="score", bufs=3)
            nc.tensor.matmul_mx(
                bank[:],
                lhsT=q_codes[:].bitcast(FP8X4),
                lhsT_scale=q_scales[:],
                rhs=k_codes[:, n].bitcast(FP8X4),
                rhs_scale=k_scales[:, n],
                start=True,
                stop=True,
            )
            return bank

        def weigh(j, bank):
            nc.vector.tensor_tensor(
                neg_a[:, j], bank[:].rearrange("q (s u) -> q u s", u=PACK), neg_ts[:, j], MULT
            )

        def least(j):
            nc.vector.tensor_reduce(
                mins[:, j : j + 1],
                neg_a[:, j].rearrange("q u s -> q (u s)"),
                axis=AXIS_X,
                op=MIN,
            )

        banks = [score(0), score(1)]
        weigh(0, banks[0])
        turn(3, 0)
        banks.append(score(2))
        least(0)
        weigh(1, banks[1])
        turn(3, 1)
        banks.append(score(3))
        least(1)
        weigh(2, banks[2])
        turn(3, 2)
        least(2)
        weigh(3, banks[3])
        turn(3, 3)
        least(3)
        nc.vector.tensor_reduce(neg_m[:], mins[:], axis=AXIS_X, op=MIN)

        p_sb = hold.tile([P, CHUNKS, PACK, P], F32, name="p_sb")
        sums = hold.tile([P, CHUNKS], F32, name="sums")
        w_grouped = hold.tile([P, CHUNKS, NQ, PACK], BF16, name="w_grouped", align_bytes=64)
        w_codes = hold.tile([P, CHUNKS, NQ], U32, name="w_codes", align_bytes=64)
        w_scales = hold.tile([P, CHUNKS, NQ], U8, name="w_scales", align_bytes=64)
        for j in range(CHUNKS):
            nc.scalar.activation(
                p_sb[:, j], neg_a[:, j], EXP, bias=neg_m[:], scale=-1.0, accum_out=sums[:, j : j + 1]
            )
        for j in range(CHUNKS):
            quantize_v(1, j)
        y = psum.tile([P, D], F32, name="y", tag="y", bufs=1)

        def turn_p(j):
            bank = psum.tile([P, PACK, P], F32, name="p_turned", tag="turned", bufs=4)
            for u in range(PACK):
                nc.tensor.transpose(bank[:, u, :], p_sb[:, j, u, :], ident[:])
            return bank

        def weights(j, bank):
            nc.vector.tensor_tensor(
                w_grouped[:, j],
                bank[:].rearrange("s u q -> s q u"),
                ts_col[:, j, :].unsqueeze(1).to_broadcast([P, NQ, PACK]),
                MULT,
            )

        def product(j):
            nc.vector.quantize_mx(
                out=w_codes[:, j, :].bitcast(FP8X4),
                scales=w_scales[:, j, :],
                in_=w_grouped[:, j].rearrange("s q u -> s (q u)"),
            )
            nc.tensor.matmul_mx(
                y[:],
                lhsT=w_codes[:, j, :].bitcast(FP8X4),
                lhsT_scale=w_scales[:, j, :],
                rhs=v_codes[:, j, :].bitcast(FP8X4),
                rhs_scale=v_scales[:, j, :],
                start=(j == 0),
                stop=(j == CHUNKS - 1),
            )

        total = hold.tile([P, 1], F32, name="total")
        share = hold.tile([P, 1], F32, name="share")
        turned = [turn_p(0), turn_p(1)]
        weights(0, turned[0])
        turned.append(turn_p(2))
        weights(1, turned[1])
        product(0)
        turned.append(turn_p(3))
        weights(2, turned[2])
        product(1)
        weights(3, turned[3])
        product(2)
        nc.vector.tensor_reduce(total[:], sums[:], axis=AXIS_X, op=ADD)
        product(3)
        nc.vector.reciprocal(share[:], total[:])

        for h, queue in enumerate((nc.sync, nc.scalar)):
            half = P // 2
            e = slice(h * D // 2, (h + 1) * D // 2)
            result = hold.tile([P, half, PACK], F32, name=f"result{h}")
            nc.vector.scalar_tensor_tensor(
                out=result[:],
                in0=y[:].rearrange("q (t p) -> q p t", t=PACK)[:, h * half : (h + 1) * half, :],
                scalar=share[:],
                in1=ch_sb[:, e].rearrange("q (p t) -> q p t", t=PACK),
                op0=MULT,
                op1=MULT,
            )
            queue.dma_start(out=out[0][:, e], in_=result[:].rearrange("q p t -> q (p t)"))
